import numpy as np
import ml_dtypes


def mxq(x, axis, fmt="e4m3"):
    dtype, down = {"e4m3": (ml_dtypes.float8_e4m3fn, 7), "e5m2": (ml_dtypes.float8_e5m2, 14)}[fmt]
    v = np.moveaxis(np.asarray(x, np.float32).astype(ml_dtypes.bfloat16).astype(np.float64), axis, -1)
    blocks = v.reshape(v.shape[:-1] + (-1, 32))
    amax = np.abs(blocks).max(-1, keepdims=True)
    byte = np.maximum(np.where(amax > 0, np.frexp(amax)[1] - 1 + 127, 0) - down, 1)
    scale = np.exp2(byte - 127.0)
    codes = (blocks / scale).astype(np.float32).astype(dtype).astype(np.float64)
    return np.moveaxis((codes * scale).reshape(v.shape), -1, axis)


WIDE = False


def mx_kscale(k):
    if not WIDE:
        return np.ones(k)
    levels = np.array([10, -10, 5, -5, 0])
    if k % 512:
        return np.exp2(np.random.permutation(np.resize(levels, k // 32))).repeat(32)
    a = np.empty((k // 512, 16))
    for p in range(k // 512):
        a[p, :8] = np.random.permutation(np.resize(levels, 8))
        for g in range(8):
            far = levels[np.abs(levels - a[p, g]) >= 10]
            a[p, g + 8] = far[np.random.randint(len(far))]
    return np.exp2(a.ravel()).repeat(32)


def f64(x):
    return np.asarray(x).astype(np.float64)


def striped(idx):
    return np.tile(idx.reshape(-1, 16).T, (8, 1)).astype(np.uint16)


def unstriped(offs):
    return offs[:16].T.reshape(-1).astype(np.int64)


def striped8(idx):
    return np.concatenate([x.reshape(-1, 16).T for x in idx]).astype(np.uint16)


def runs(offs, k):
    lists = np.stack([offs[16 * r : 16 * r + 16].T.reshape(-1) for r in range(8)]).astype(np.int64)
    return lists[np.arange(k) % 512 // 64]


def pack_weight(w):
    k, n = w.shape
    w = f64(np.asarray(w, np.float32).astype(ml_dtypes.bfloat16)).reshape(k // 32, 32, n)
    amax = np.abs(w).max(1)
    byte = np.clip(np.where(amax > 0, np.frexp(amax)[1] - 1 + 127 - 7, 1), 1, 254)
    scaled = (w * np.exp2(127.0 - byte)[:, None, :]).reshape(k, n).astype(np.float32)
    words = np.ascontiguousarray(scaled.reshape(k // 512, 128, 4, n).transpose(0, 1, 3, 2)).astype(ml_dtypes.float8_e4m3fn).view(np.uint8)
    return words, np.ascontiguousarray(byte.astype(np.uint8).reshape(k // 512, 16, n))


def unpack_weight(words, scales):
    g, p, n, _ = words.shape
    vals = np.ascontiguousarray(words).view(ml_dtypes.float8_e4m3fn).astype(np.float64) * np.repeat(np.exp2(scales.astype(np.float64) - 127.0), 8, axis=1)[..., None]
    return vals.transpose(0, 1, 3, 2).reshape(g * 512, n)


E2M1 = np.array([0.0, 0.5, 1.0, 1.5, 2.0, 3.0, 4.0, 6.0, -0.0, -0.5, -1.0, -1.5, -2.0, -3.0, -4.0, -6.0])


def pack_fp4(w):
    k, n = w.shape
    w = f64(np.asarray(w, np.float32).astype(ml_dtypes.bfloat16)).reshape(k // 32, 32, n)
    amax = np.abs(w).max(1)
    mant, ex = np.frexp(amax / 6.0)
    byte = np.clip(np.where(amax > 0, np.where(mant > 0.5, ex, ex - 1) + 127, 1), 1, 254)
    scaled = (w * np.exp2(127.0 - byte)[:, None, :]).reshape(k, n).astype(np.float32)
    c = np.ascontiguousarray(scaled.reshape(k // 512, 128, 4, n).transpose(0, 1, 3, 2)).astype(ml_dtypes.float4_e2m1fn).view(np.uint8) & 0xF
    words = (c[..., 0::2] | (c[..., 1::2] << 4)).reshape(k // 512, 128, 2 * n)
    return np.ascontiguousarray(words), np.ascontiguousarray(byte.astype(np.uint8).reshape(k // 512, 16, n))


def unpack_fp4(words, scales):
    g, _, n = scales.shape
    words = np.ascontiguousarray(words).reshape(g, 128, n, 2)
    nib = np.empty((g, 128, n, 4), np.uint8)
    nib[..., 0::2] = words & 0xF
    nib[..., 1::2] = words >> 4
    vals = E2M1[nib] * np.repeat(np.exp2(scales.astype(np.float64) - 127.0), 8, axis=1)[..., None]
    return vals.transpose(0, 1, 3, 2).reshape(g * 512, n)


def planes(y):
    n, m = y.shape
    v = y.astype(np.float32).astype(ml_dtypes.bfloat16).astype(np.float64).reshape(n // 32, 32, m)
    top = np.abs(v).max(1)
    byte = np.clip(np.where(top > 0, np.frexp(top)[1] - 1 + 127 - 7, 1), 1, 254)
    codes = (v * np.exp2(127.0 - byte)[:, None, :]).reshape(n, m).astype(np.float32).astype(ml_dtypes.float8_e4m3fn).view(np.uint8)
    words = codes.reshape(n // 512, 128, 4, m).transpose(0, 1, 3, 2)
    return np.ascontiguousarray(words), np.ascontiguousarray(byte.astype(np.uint8).reshape(n // 512, 16, m))


K, T, S, H, C, G, W = 512, 1024, 512, 512, 512, 2048, 256


def setup_inputs():
    n = np.random.standard_normal
    s = mx_kscale(K)[:, None]
    packed_xT = pack_weight(n((K, T)) * s)
    packed_w1 = pack_fp4(n((K, H)) / np.sqrt(K) / s)
    packed_dT = pack_weight(n((K, G)) / s)
    return {
        "x_words": packed_xT[0],
        "x_scales": packed_xT[1],
        "w1_words": packed_w1[0],
        "w1_scales": packed_w1[1],
        "gs": (np.random.uniform(0.5, 1.5, (K, 1)) / s).astype(np.float32),
        "gk": (np.random.uniform(0.5, 1.5, (K, 1)) * s).astype(np.float32),
        "d_words": packed_dT[0],
        "d_scales": packed_dT[1],
        "offs": striped(np.random.permutation(T)[:S]),
        "n1": striped8(np.stack([np.random.permutation(S) for _ in range(8)])),
        "n2": striped8(np.stack([np.random.permutation(S) for _ in range(8)])),
        "n3": striped(np.random.permutation(S)),
        "n4": striped(np.random.permutation(S)),
        "cand": striped(np.random.permutation(T)[:C]),
        "k1": striped8(np.random.randint(0, G, (8, H))),
        "n5": striped(np.random.permutation(S)[:W]),
        "n6": striped(np.random.permutation(S)[:W]),
    }


def reference(x_words, x_scales, w1_words, w1_scales, gs, gk, d_words, d_scales, offs, n1, n2, n3, n4, cand, k1, n5, n6):
    d_k1 = unpack_weight(d_words, d_scales)[np.arange(K)[:, None], runs(k1, K)]
    xq = unpack_weight(x_words, x_scales)[:, unstriped(offs)]
    y = unpack_fp4(w1_words, w1_scales).T @ xq
    z2 = f64(gk) * (y[:, unstriped(n3)] + 0.75 * y[:, unstriped(n4)])
    b = 0.0625 * ((d_k1.T @ mxq(z2, 0, "e4m3")))
    x_cand = unpack_weight(x_words, x_scales)[:, unstriped(cand)]
    z = f64(gs) * (0.75 * ((y - (y[np.arange(H)[:, None], runs(n1, H)])) * (y - (y[np.arange(H)[:, None], runs(n2, H)]))))
    a = 0.0625 * ((x_cand.T @ mxq(z, 0, "e4m3")))
    ra = b[:, unstriped(n6)] - (0.5 * a[:, unstriped(n5)])
    out = a.copy()
    out[:, unstriped(n5)] = ra
    return (out,) + planes(out)

@@ -1,0 +1,210 @@
+from contextlib import ExitStack
+
+import concourse.mybir as mybir
+
+F32 = mybir.dt.float32
+BF16 = mybir.dt.bfloat16
+I32 = mybir.dt.int32
+U32 = mybir.dt.uint32
+U16 = mybir.dt.uint16
+U8 = mybir.dt.uint8
+FP8X4 = mybir.dt.float8_e4m3fn_x4
+FP4X4 = mybir.dt.float4_e2m1fn_x4
+ADD = mybir.AluOpType.add
+SUB = mybir.AluOpType.subtract
+MULT = mybir.AluOpType.mult
+COPY = mybir.ActivationFunctionType.Copy
+
+P = 128
+T4 = 4
+T, S, G, W = 1024, 512, 2048, 256
+FLOPS = 3 * 2 * 512 * 512 * 512
+
+
+def tile_picked_cdkeyputbquadsum_none_po_kernel(
+    tc, x_words, x_scales, w1_words, w1_scales, gs, gk, d_words, d_scales,
+    offs, n1, n2, n3, n4, cand, k1, n5, n6, out_0, out_1, out_2,
+):
+    nc = tc.nc
+    with ExitStack() as ctx:
+        pool = ctx.enter_context(tc.tile_pool(name="held", bufs=1))
+        psum = ctx.enter_context(tc.psum_pool(name="psum", bufs=1))
+
+        def sb(name, shape, dtype):
+            return pool.tile(shape, dtype, name=name, align_bytes=64)
+
+        def load_list(name, src):
+            lst = pool.tile(list(src.shape), U16, name=name)
+            nc.sync.dma_start(lst[:], src)
+            return lst
+
+        def load_scales(dst, src):
+            for r in range(4):
+                nc.sync.dma_start(dst[r:P:32, :].bitcast(I32), src[0, r:16:4, :].bitcast(I32))
+
+        x_sc = sb("x_sc", [P, T], U8)
+        w_sc = sb("w_sc", [P, S], U8)
+        d_sc = sb("d_sc", [P, G], U8)
+        key_sc = sb("key_sc", [P, S], U8)
+        nc.vector.memset(x_sc[:].bitcast(I32), 0)
+        nc.vector.memset(w_sc[:].bitcast(I32), 0)
+        nc.gpsimd.memset(d_sc[:].bitcast(I32), 0)
+        nc.gpsimd.memset(key_sc[:].bitcast(I32), 0)
+
+        offs_l = load_list("offs_l", offs)
+        w_wd = sb("w_wd", [P, 2 * S], U8)
+        nc.sync.dma_start(w_wd[:].bitcast(I32), w1_words[0].bitcast(I32))
+        load_scales(x_sc, x_scales)
+        x_wd = sb("x_wd", [P, T], U32)
+        nc.sync.dma_start(x_wd[:].bitcast(I32), x_words[0].rearrange("p c r -> p (c r)").bitcast(I32))
+        load_scales(w_sc, w1_scales)
+        cand_l = load_list("cand_l", cand)
+        gs4 = sb("gs4", [P, T4], F32)
+        gk4 = sb("gk4", [P, T4], F32)
+        nc.sync.dma_start(gs4[:], gs.rearrange("(p t) o -> p (t o)", t=T4))
+        nc.sync.dma_start(gk4[:], gk.rearrange("(p t) o -> p (t o)", t=T4))
+        k1_l = load_list("k1_l", k1)
+        for e in range(2):
+            nc.sync.dma_start(d_sc[e:P:16, :].bitcast(I32), d_scales[0, e:16:2, :].bitcast(I32))
+        n1_l = load_list("n1_l", n1)
+        n2_l = load_list("n2_l", n2)
+        n3_l = load_list("n3_l", n3)
+        n4_l = load_list("n4_l", n4)
+        d_wd = sb("d_wd", [P, G], U32)
+        nc.sync.dma_start(d_wd[:].bitcast(I32), d_words[0].rearrange("p c r -> p (c r)").bitcast(I32))
+        n5_l = load_list("n5_l", n5)
+        n6_l = load_list("n6_l", n6)
+
+        gs75 = sb("gs75", [P, T4], F32)
+        nc.gpsimd.tensor_scalar(gs75[:], gs4[:], 0.75, 0.0, MULT, ADD)
+
+        def gather(name, window, lst, dtype):
+            got = sb(name, [P, S], dtype)
+            nc.vector.tensor_copy(got[:], window[:].indirect(lst[:]))
+            return got
+
+        def deal_words(name, src):
+            dst = sb(name, [P, S], U32)
+            nc.vector.tensor_copy(dst[:].rearrange("p (t m) -> p m t", t=T4), src[:].rearrange("p (m t) -> p m t", t=T4))
+            return dst
+
+        def deal_bytes(name, src):
+            dst = sb(name, [P, S], U8)
+            nc.vector.tensor_copy(dst[:].rearrange("p (t m) -> p t m", t=T4), src[:].rearrange("p (m t) -> p t m", t=T4))
+            return dst
+
+        xq_sc = gather("xq_sc", x_sc, offs_l, U8)
+        w_wd_d = sb("w_wd_d", [P, 2 * S], U8)
+        nc.vector.tensor_copy(
+            w_wd_d[:].rearrange("p (t m b) -> p t m b", t=T4, b=2), w_wd[:].rearrange("p (m t b) -> p t m b", t=T4, b=2))
+        xq_wd = gather("xq_wd", x_wd, offs_l, U32)
+        w_sc_d = deal_bytes("w_sc_d", w_sc)
+
+        y_ps = [psum.tile([P, S], F32, name="y_ps%d" % t, tag="low%d" % t) for t in range(T4)]
+        for t in range(T4):
+            nc.tensor.matmul_mx(
+                out=y_ps[t][:], lhsT=w_wd_d[:, 2 * P * t:2 * P * (t + 1)].bitcast(FP4X4), lhsT_scale=w_sc_d[:, P * t:P * (t + 1)],
+                rhs=xq_wd[:].bitcast(FP8X4), rhs_scale=xq_sc[:], start=True, stop=True)
+
+        y_yk = [sb("y_yk%d" % t, [P, 2 * S], F32) for t in range(T4)]
+        ys_y = [sb("ys_y%d" % t, [P, 2 * S], F32) for t in range(T4)]
+        ys2 = [sb("ys2_%d" % t, [P, S], F32) for t in range(T4)]
+        for t in range(T4):
+            nc.scalar.activation(y_yk[t][:, :S], y_ps[t][:], COPY)
+            nc.sync.dma_start(ys_y[t][:, S:], y_yk[t][:, :S])
+            nc.scalar.activation(ys_y[t][:, :S], y_ps[t][:], COPY, scale=gs75[:, t:t + 1])
+            nc.sync.dma_start(ys2[t][:], ys_y[t][:, :S])
+            nc.scalar.activation(y_yk[t][:, S:], y_ps[t][:], COPY, scale=gk4[:, t:t + 1])
+
+        cand_sc = deal_bytes("cand_sc", gather("cand_sc_g", x_sc, cand_l, U8))
+        cand_wd = deal_words("cand_wd", gather("cand_wd_g", x_wd, cand_l, U32))
+        key_sc_d = deal_bytes("key_sc_d", gather("key_sc_g", d_sc, k1_l, U8))
+        for i, src in enumerate((0, 1, 16, 17)):
+            nc.sync.dma_start(key_sc[i:P:32, :].bitcast(I32), key_sc_d[src:P:32, :].bitcast(I32))
+
+        d1 = sb("d1", [P, T4, S], F32)
+        d2 = sb("d2", [P, T4, S], F32)
+        g3 = sb("g3", [P, T4, S], F32)
+        g4 = sb("g4", [P, T4, S], F32)
+        for t in range(T4):
+            nc.vector.tensor_tensor(d1[:, t, :], ys_y[t][:].indirect(n1_l[:]), ys2[t][:], SUB)
+            nc.vector.tensor_tensor(d2[:, t, :], y_yk[t][:].indirect(n2_l[:]), ys_y[t][:, S:], SUB)
+        for t in range(T4):
+            for h in range(2):
+                cols = slice(W * h, W * (h + 1))
+                lc = slice(16 * h, 16 * (h + 1))
+                nc.scalar.activation(g3[:, t, cols], y_yk[t][:, S:].indirect(n3_l[:, lc]), COPY)
+                nc.scalar.activation(g4[:, t, cols], y_yk[t][:, S:].indirect(n4_l[:, lc]), COPY, scale=0.75)
+
+        def woven(tile3):
+            return tile3[:].rearrange("p t (c i) -> p c t i", i=4)
+
+        def woven_out(tile3):
+            return tile3[:].rearrange("p (c i) t -> p c t i", i=4)
+
+        def quantize(name, src):
+            wd = sb(name + "_wd", [P, S], U32)
+            sc = sb(name + "_sc", [P, S], U8)
+            nc.vector.quantize_mx(out=wd[:].bitcast(FP8X4), scales=sc[:], in_=src[:].rearrange("p c t -> p (c t)"))
+            return wd, sc
+
+        def product(name, tag, lw, ls, rw, rs):
+            res = [psum.tile([P, S], F32, name="%s%d" % (name, t), tag="%s%d" % (tag, t)) for t in range(T4)]
+            for t in range(T4):
+                cols = slice(P * t, P * (t + 1))
+                nc.tensor.matmul_mx(out=res[t][:], lhsT=lw[:, cols].bitcast(FP8X4), lhsT_scale=ls[:, cols],
+                                    rhs=rw[:].bitcast(FP8X4), rhs_scale=rs[:], start=True, stop=True)
+            return res
+
+        z_bf = sb("z_bf", [P, S, T4], BF16)
+        nc.vector.tensor_tensor(woven_out(z_bf), woven(d1), woven(d2), MULT)
+        key_wd_g = gather("key_wd_g", d_wd, k1_l, U32)
+        z_wd, z_sc = quantize("z", z_bf)
+        a_ps = product("a_ps", "high", cand_wd, cand_sc, z_wd, z_sc)
+
+        z2_bf = sb("z2_bf", [P, S, T4], BF16)
+        nc.vector.tensor_tensor(woven_out(z2_bf), woven(g3), woven(g4), ADD)
+        key_wd = deal_words("key_wd", key_wd_g)
+        z2_wd, z2_sc = quantize("z2", z2_bf)
+        b_ps = product("b_ps", "low", key_wd, key_sc, z2_wd, z2_sc)
+
+        a_sb = [sb("a_sb%d" % t, [P, S], F32) for t in range(T4)]
+        b_sb = [sb("b_sb%d" % t, [P, S], F32) for t in range(T4)]
+        half = [sb("half%d" % t, [P, W], F32) for t in range(T4)]
+        ra = [sb("ra%d" % t, [P, W], F32) for t in range(T4)]
+        for t in range(T4):
+            nc.scalar.activation(a_sb[t][:], a_ps[t][:], COPY, scale=0.0625)
+            nc.scalar.activation(half[t][:], a_sb[t][:].indirect(n5_l[:]), COPY, scale=0.5)
+        o_all = sb("o_all", [P, T4, S], F32)
+        out_rows = out_0.rearrange("(p t) c -> p t c", t=T4)
+        for t in range(T4):
+            if t % 2 == 0:
+                nc.vector.tensor_scalar(b_sb[t][:], b_ps[t][:], 0.0625, None, MULT)
+            else:
+                nc.scalar.activation(b_sb[t][:], b_ps[t][:], COPY, scale=0.0625)
+            nc.vector.tensor_tensor(ra[t][:], b_sb[t][:].indirect(n6_l[:]), half[t][:], SUB)
+        for t in range(T4):
+            if t % 2 == 0:
+                nc.scalar.activation(a_sb[t][:].indirect(n5_l[:]), ra[t][:], COPY)
+            else:
+                nc.vector.tensor_copy(a_sb[t][:].indirect(n5_l[:]), ra[t][:])
+            if t < 2:
+                nc.sync.dma_start(o_all[:, t, :], a_sb[t][:])
+            elif t == 2:
+                nc.scalar.activation(o_all[:, t, :], a_sb[t][:], COPY)
+            else:
+                nc.vector.tensor_copy(o_all[:, t, :], a_sb[t][:])
+            nc.sync.dma_start(out_rows[:, t, :], a_sb[t][:])
+
+        o_bf = sb("o_bf", [P, S, T4], BF16)
+        nc.vector.tensor_copy(woven_out(o_bf)[:, :64], woven(o_all)[:, :64])
+        nc.scalar.activation(woven_out(o_bf)[:, 64:], woven(o_all)[:, 64:], COPY)
+        o_wd = sb("o_wd", [P, S], U32)
+        o_sc = sb("o_sc", [P, S], U8)
+        words_out = out_1[0].rearrange("p c r -> p (c r)").bitcast(I32)
+        for h in range(2):
+            cols = slice(W * h, W * (h + 1))
+            nc.vector.quantize_mx(out=o_wd[:, cols].bitcast(FP8X4), scales=o_sc[:, cols], in_=o_bf[:, cols, :].rearrange("p c t -> p (c t)"))
+            nc.sync.dma_start(words_out[:, cols], o_wd[:, cols].bitcast(I32))
+        for r in range(4):
+            nc.sync.dma_start(out_2[0, r:16:4, :].bitcast(I32), o_sc[r:P:32, :].bitcast(I32))

@@ -30,8 +30,8 @@ def tile_picked_cdkeyputbquadsum_none_po_kernel(
         pool = ctx.enter_context(tc.tile_pool(name="held", bufs=1))
         psum = ctx.enter_context(tc.psum_pool(name="psum", bufs=1))
 
-        def sb(name, shape, dtype):
-            return pool.tile(shape, dtype, name=name, align_bytes=64)
+        def sb(name, shape, dtype, tag=None):
+            return pool.tile(shape, dtype, name=name, tag=tag or name, align_bytes=64)
 
         def load_list(name, src):
             lst = pool.tile(list(src.shape), U16, name=name)
@@ -46,8 +46,8 @@ def tile_picked_cdkeyputbquadsum_none_po_kernel(
         w_sc = sb("w_sc", [P, S], U8)
         d_sc = sb("d_sc", [P, G], U8)
         key_sc = sb("key_sc", [P, S], U8)
-        nc.vector.memset(x_sc[:].bitcast(I32), 0)
-        nc.vector.memset(w_sc[:].bitcast(I32), 0)
+        nc.gpsimd.memset(x_sc[:].bitcast(I32), 0)
+        nc.gpsimd.memset(w_sc[:].bitcast(I32), 0)
         nc.gpsimd.memset(d_sc[:].bitcast(I32), 0)
         nc.gpsimd.memset(key_sc[:].bitcast(I32), 0)
 
@@ -78,8 +78,8 @@ def tile_picked_cdkeyputbquadsum_none_po_kernel(
         gs75 = sb("gs75", [P, T4], F32)
         nc.gpsimd.tensor_scalar(gs75[:], gs4[:], 0.75, 0.0, MULT, ADD)
 
-        def gather(name, window, lst, dtype):
-            got = sb(name, [P, S], dtype)
+        def gather(name, window, lst, dtype, tag=None):
+            got = sb(name, [P, S], dtype, tag)
             nc.vector.tensor_copy(got[:], window[:].indirect(lst[:]))
             return got
 
@@ -94,27 +94,29 @@ def tile_picked_cdkeyputbquadsum_none_po_kernel(
             return dst
 
         xq_sc = gather("xq_sc", x_sc, offs_l, U8)
-        w_wd_d = sb("w_wd_d", [P, 2 * S], U8)
-        nc.vector.tensor_copy(
-            w_wd_d[:].rearrange("p (t m b) -> p t m b", t=T4, b=2), w_wd[:].rearrange("p (m t b) -> p t m b", t=T4, b=2))
         xq_wd = gather("xq_wd", x_wd, offs_l, U32)
-        w_sc_d = deal_bytes("w_sc_d", w_sc)
-
         y_ps = [psum.tile([P, S], F32, name="y_ps%d" % t, tag="low%d" % t) for t in range(T4)]
         for t in range(T4):
+            w_wd_t = sb("w_wd_%d" % t, [P, 2 * P], U8)
+            w_sc_t = sb("w_sc_%d" % t, [P, P], U8)
+            nc.vector.tensor_copy(w_wd_t[:].rearrange("p (m b) -> p m b", b=2), w_wd[:].rearrange("p (m t b) -> p t m b", t=T4, b=2)[:, t])
+            nc.vector.tensor_copy(w_sc_t[:], w_sc[:, t:S:T4])
             nc.tensor.matmul_mx(
-                out=y_ps[t][:], lhsT=w_wd_d[:, 2 * P * t:2 * P * (t + 1)].bitcast(FP4X4), lhsT_scale=w_sc_d[:, P * t:P * (t + 1)],
+                out=y_ps[t][:], lhsT=w_wd_t[:].bitcast(FP4X4), lhsT_scale=w_sc_t[:],
                 rhs=xq_wd[:].bitcast(FP8X4), rhs_scale=xq_sc[:], start=True, stop=True)
 
-        y_yk = [sb("y_yk%d" % t, [P, 2 * S], F32) for t in range(T4)]
+        y_ys = [sb("y_ys%d" % t, [P, 2 * S], F32) for t in range(T4)]
         ys_y = [sb("ys_y%d" % t, [P, 2 * S], F32) for t in range(T4)]
-        ys2 = [sb("ys2_%d" % t, [P, S], F32) for t in range(T4)]
+        yk = [sb("yk%d" % t, [P, S + 16], F32) for t in range(T4)]
         for t in range(T4):
-            nc.scalar.activation(y_yk[t][:, :S], y_ps[t][:], COPY)
-            nc.sync.dma_start(ys_y[t][:, S:], y_yk[t][:, :S])
+            nc.gpsimd.memset(yk[t][:, S:], 0.0)
+        for t in range(T4):
+            nc.scalar.activation(y_ys[t][:, :S], y_ps[t][:], COPY)
+            nc.sync.dma_start(ys_y[t][:, S:], y_ys[t][:, :S])
             nc.scalar.activation(ys_y[t][:, :S], y_ps[t][:], COPY, scale=gs75[:, t:t + 1])
-            nc.sync.dma_start(ys2[t][:], ys_y[t][:, :S])
-            nc.scalar.activation(y_yk[t][:, S:], y_ps[t][:], COPY, scale=gk4[:, t:t + 1])
+            nc.sync.dma_start(y_ys[t][:, S:], ys_y[t][:, :S])
+        for t in range(T4):
+            nc.scalar.activation(yk[t][:, :S], y_ps[t][:], COPY, scale=gk4[:, t:t + 1])
 
         cand_sc = deal_bytes("cand_sc", gather("cand_sc_g", x_sc, cand_l, U8))
         cand_wd = deal_words("cand_wd", gather("cand_wd_g", x_wd, cand_l, U32))
@@ -127,25 +129,31 @@ def tile_picked_cdkeyputbquadsum_none_po_kernel(
         g3 = sb("g3", [P, T4, S], F32)
         g4 = sb("g4", [P, T4, S], F32)
         for t in range(T4):
-            nc.vector.tensor_tensor(d1[:, t, :], ys_y[t][:].indirect(n1_l[:]), ys2[t][:], SUB)
-            nc.vector.tensor_tensor(d2[:, t, :], y_yk[t][:].indirect(n2_l[:]), ys_y[t][:, S:], SUB)
+            nc.vector.tensor_tensor(d1[:, t, :], ys_y[t][:].indirect(n1_l[:]), y_ys[t][:, S:], SUB)
+            nc.vector.tensor_tensor(d2[:, t, :], y_ys[t][:].indirect(n2_l[:]), ys_y[t][:, S:], SUB)
         for t in range(T4):
+            nc.scalar.activation(g3[:, t, :], yk[t][:].indirect(n3_l[:]), COPY)
+            nc.scalar.activation(g4[:, t, :], yk[t][:].indirect(n4_l[:]), COPY, scale=0.75)
+
+        def woven(planes):
+            return planes.rearrange("p t (c i) -> p c t i", i=4)
+
+        def woven_out(words):
+            return words.rearrange("p (c i) t -> p c t i", i=4)
+
+        halves = [slice(W * h, W * (h + 1)) for h in range(2)]
+
+        def weave(name, tags, in0, in1, op):
+            out = [sb("%s%d" % (name, h), [P, W, T4], BF16, tags[h]) for h in range(2)]
             for h in range(2):
-                cols = slice(W * h, W * (h + 1))
-                lc = slice(16 * h, 16 * (h + 1))
-                nc.scalar.activation(g3[:, t, cols], y_yk[t][:, S:].indirect(n3_l[:, lc]), COPY)
-                nc.scalar.activation(g4[:, t, cols], y_yk[t][:, S:].indirect(n4_l[:, lc]), COPY, scale=0.75)
-
-        def woven(tile3):
-            return tile3[:].rearrange("p t (c i) -> p c t i", i=4)
-
-        def woven_out(tile3):
-            return tile3[:].rearrange("p (c i) t -> p c t i", i=4)
+                nc.vector.tensor_tensor(woven_out(out[h][:]), woven(in0[:, :, halves[h]]), woven(in1[:, :, halves[h]]), op)
+            return out
 
         def quantize(name, src):
             wd = sb(name + "_wd", [P, S], U32)
             sc = sb(name + "_sc", [P, S], U8)
-            nc.vector.quantize_mx(out=wd[:].bitcast(FP8X4), scales=sc[:], in_=src[:].rearrange("p c t -> p (c t)"))
+            for h in range(2):
+                nc.vector.quantize_mx(out=wd[:, halves[h]].bitcast(FP8X4), scales=sc[:, halves[h]], in_=src[h][:].rearrange("p c t -> p (c t)"))
             return wd, sc
 
         def product(name, tag, lw, ls, rw, rs):
@@ -156,14 +164,12 @@ def tile_picked_cdkeyputbquadsum_none_po_kernel(
                                     rhs=rw[:].bitcast(FP8X4), rhs_scale=rs[:], start=True, stop=True)
             return res
 
-        z_bf = sb("z_bf", [P, S, T4], BF16)
-        nc.vector.tensor_tensor(woven_out(z_bf), woven(d1), woven(d2), MULT)
-        key_wd_g = gather("key_wd_g", d_wd, k1_l, U32)
+        z_bf = weave("z_bf", ("z_bf0", "z_bf1"), d1, d2, MULT)
         z_wd, z_sc = quantize("z", z_bf)
         a_ps = product("a_ps", "high", cand_wd, cand_sc, z_wd, z_sc)
 
-        z2_bf = sb("z2_bf", [P, S, T4], BF16)
-        nc.vector.tensor_tensor(woven_out(z2_bf), woven(g3), woven(g4), ADD)
+        key_wd_g = gather("key_wd_g", d_wd, k1_l, U32, "z_bf0")
+        z2_bf = weave("z2_bf", ("z_bf1", "d1"), g3, g4, ADD)
         key_wd = deal_words("key_wd", key_wd_g)
         z2_wd, z2_sc = quantize("z2", z2_bf)
         b_ps = product("b_ps", "low", key_wd, key_sc, z2_wd, z2_sc)
@@ -178,13 +184,10 @@ def tile_picked_cdkeyputbquadsum_none_po_kernel(
         o_all = sb("o_all", [P, T4, S], F32)
         out_rows = out_0.rearrange("(p t) c -> p t c", t=T4)
         for t in range(T4):
-            if t % 2 == 0:
-                nc.vector.tensor_scalar(b_sb[t][:], b_ps[t][:], 0.0625, None, MULT)
-            else:
-                nc.scalar.activation(b_sb[t][:], b_ps[t][:], COPY, scale=0.0625)
+            nc.vector.tensor_scalar(b_sb[t][:], b_ps[t][:], 0.0625, None, MULT)
             nc.vector.tensor_tensor(ra[t][:], b_sb[t][:].indirect(n6_l[:]), half[t][:], SUB)
         for t in range(T4):
-            if t % 2 == 0:
+            if t < 3:
                 nc.scalar.activation(a_sb[t][:].indirect(n5_l[:]), ra[t][:], COPY)
             else:
                 nc.vector.tensor_copy(a_sb[t][:].indirect(n5_l[:]), ra[t][:])
@@ -197,14 +200,14 @@ def tile_picked_cdkeyputbquadsum_none_po_kernel(
             nc.sync.dma_start(out_rows[:, t, :], a_sb[t][:])
 
         o_bf = sb("o_bf", [P, S, T4], BF16)
-        nc.vector.tensor_copy(woven_out(o_bf)[:, :64], woven(o_all)[:, :64])
-        nc.scalar.activation(woven_out(o_bf)[:, 64:], woven(o_all)[:, 64:], COPY)
+        parts = [slice(0, 384), slice(384, S)]
+        nc.vector.tensor_copy(woven_out(o_bf[:, parts[0], :]), woven(o_all[:, :, parts[0]]))
+        nc.scalar.activation(o_bf[:, parts[1], :], o_all[:, :, parts[1]].rearrange("p t c -> p c t"), COPY)
         o_wd = sb("o_wd", [P, S], U32)
         o_sc = sb("o_sc", [P, S], U8)
         words_out = out_1[0].rearrange("p c r -> p (c r)").bitcast(I32)
-        for h in range(2):
-            cols = slice(W * h, W * (h + 1))
+        for cols in reversed(parts):
             nc.vector.quantize_mx(out=o_wd[:, cols].bitcast(FP8X4), scales=o_sc[:, cols], in_=o_bf[:, cols, :].rearrange("p c t -> p (c t)"))
-            nc.sync.dma_start(words_out[:, cols], o_wd[:, cols].bitcast(I32))
+        nc.scalar.dma_start(words_out, o_wd[:].bitcast(I32))
         for r in range(4):
             nc.sync.dma_start(out_2[0, r:16:4, :].bitcast(I32), o_sc[r:P:32, :].bitcast(I32))

@@ -108,18 +108,21 @@ def tile_picked_cdkeyputbquadsum_none_po_kernel(
         y_ys = [sb("y_ys%d" % t, [P, 2 * S], F32) for t in range(T4)]
         ys_y = [sb("ys_y%d" % t, [P, 2 * S], F32) for t in range(T4)]
         yk = [sb("yk%d" % t, [P, S + 16], F32) for t in range(T4)]
+        ys2 = [sb("ys2_0", [P, S], F32)[:]] + [y_ys[t][:, S:] for t in range(1, T4)]
+        nc.gpsimd.memset(y_ys[0][:, S:], 0.0)
         for t in range(T4):
             nc.gpsimd.memset(yk[t][:, S:], 0.0)
         for t in range(T4):
             nc.scalar.activation(y_ys[t][:, :S], y_ps[t][:], COPY)
             nc.sync.dma_start(ys_y[t][:, S:], y_ys[t][:, :S])
             nc.scalar.activation(ys_y[t][:, :S], y_ps[t][:], COPY, scale=gs75[:, t:t + 1])
-            nc.sync.dma_start(y_ys[t][:, S:], ys_y[t][:, :S])
+            nc.sync.dma_start(ys2[t], ys_y[t][:, :S])
         for t in range(T4):
             nc.scalar.activation(yk[t][:, :S], y_ps[t][:], COPY, scale=gk4[:, t:t + 1])
 
         cand_sc = deal_bytes("cand_sc", gather("cand_sc_g", x_sc, cand_l, U8))
         cand_wd = deal_words("cand_wd", gather("cand_wd_g", x_wd, cand_l, U32))
+
         key_sc_d = deal_bytes("key_sc_d", gather("key_sc_g", d_sc, k1_l, U8))
         for i, src in enumerate((0, 1, 16, 17)):
             nc.sync.dma_start(key_sc[i:P:32, :].bitcast(I32), key_sc_d[src:P:32, :].bitcast(I32))
@@ -129,8 +132,8 @@ def tile_picked_cdkeyputbquadsum_none_po_kernel(
         g3 = sb("g3", [P, T4, S], F32)
         g4 = sb("g4", [P, T4, S], F32)
         for t in range(T4):
-            nc.vector.tensor_tensor(d1[:, t, :], ys_y[t][:].indirect(n1_l[:]), y_ys[t][:, S:], SUB)
             nc.vector.tensor_tensor(d2[:, t, :], y_ys[t][:].indirect(n2_l[:]), ys_y[t][:, S:], SUB)
+            nc.vector.tensor_tensor(d1[:, t, :], ys_y[t][:].indirect(n1_l[:]), ys2[t], SUB)
         for t in range(T4):
             nc.scalar.activation(g3[:, t, :], yk[t][:].indirect(n3_l[:]), COPY)
             nc.scalar.activation(g4[:, t, :], yk[t][:].indirect(n4_l[:]), COPY, scale=0.75)
@@ -160,8 +163,9 @@ def tile_picked_cdkeyputbquadsum_none_po_kernel(
             res = [psum.tile([P, S], F32, name="%s%d" % (name, t), tag="%s%d" % (tag, t)) for t in range(T4)]
             for t in range(T4):
                 cols = slice(P * t, P * (t + 1))
-                nc.tensor.matmul_mx(out=res[t][:], lhsT=lw[:, cols].bitcast(FP8X4), lhsT_scale=ls[:, cols],
-                                    rhs=rw[:].bitcast(FP8X4), rhs_scale=rs[:], start=True, stop=True)
+                for n in halves:
+                    nc.tensor.matmul_mx(out=res[t][:, n], lhsT=lw[:, cols].bitcast(FP8X4), lhsT_scale=ls[:, cols],
+                                        rhs=rw[:, n].bitcast(FP8X4), rhs_scale=rs[:, n], start=True, stop=True)
             return res
 
         z_bf = weave("z_bf", ("z_bf0", "z_bf1"), d1, d2, MULT)
@@ -175,16 +179,21 @@ def tile_picked_cdkeyputbquadsum_none_po_kernel(
         b_ps = product("b_ps", "low", key_wd, key_sc, z2_wd, z2_sc)
 
         a_sb = [sb("a_sb%d" % t, [P, S], F32) for t in range(T4)]
-        b_sb = [sb("b_sb%d" % t, [P, S], F32) for t in range(T4)]
+        b_sb = [sb("b_sb%d" % t, [P, S], F32, "b_sb%d" % (t % 2)) for t in range(T4)]
         half = [sb("half%d" % t, [P, W], F32) for t in range(T4)]
         ra = [sb("ra%d" % t, [P, W], F32) for t in range(T4)]
-        for t in range(T4):
+        last = T4 - 1
+        for t in range(last):
             nc.scalar.activation(a_sb[t][:], a_ps[t][:], COPY, scale=0.0625)
             nc.scalar.activation(half[t][:], a_sb[t][:].indirect(n5_l[:]), COPY, scale=0.5)
+        nc.vector.tensor_scalar(a_sb[last][:], a_ps[last][:], 0.0625, None, MULT)
+        nc.scalar.activation(b_sb[0][:], b_ps[0][:], COPY, scale=0.0625)
+        nc.scalar.activation(half[last][:], a_sb[last][:].indirect(n5_l[:]), COPY, scale=0.5)
         o_all = sb("o_all", [P, T4, S], F32)
         out_rows = out_0.rearrange("(p t) c -> p t c", t=T4)
         for t in range(T4):
-            nc.vector.tensor_scalar(b_sb[t][:], b_ps[t][:], 0.0625, None, MULT)
+            if t > 0:
+                nc.vector.tensor_scalar(b_sb[t][:], b_ps[t][:], 0.0625, None, MULT)
             nc.vector.tensor_tensor(ra[t][:], b_sb[t][:].indirect(n6_l[:]), half[t][:], SUB)
         for t in range(T4):
             if t < 3:
@@ -193,21 +202,18 @@ def tile_picked_cdkeyputbquadsum_none_po_kernel(
                 nc.vector.tensor_copy(a_sb[t][:].indirect(n5_l[:]), ra[t][:])
             if t < 2:
                 nc.sync.dma_start(o_all[:, t, :], a_sb[t][:])
-            elif t == 2:
-                nc.scalar.activation(o_all[:, t, :], a_sb[t][:], COPY)
-            else:
-                nc.vector.tensor_copy(o_all[:, t, :], a_sb[t][:])
             nc.sync.dma_start(out_rows[:, t, :], a_sb[t][:])
+        for t in (3, 2):
+            nc.vector.tensor_copy(o_all[:, t, :], a_sb[t][:])
 
-        o_bf = sb("o_bf", [P, S, T4], BF16)
-        parts = [slice(0, 384), slice(384, S)]
-        nc.vector.tensor_copy(woven_out(o_bf[:, parts[0], :]), woven(o_all[:, :, parts[0]]))
-        nc.scalar.activation(o_bf[:, parts[1], :], o_all[:, :, parts[1]].rearrange("p t c -> p c t"), COPY)
-        o_wd = sb("o_wd", [P, S], U32)
-        o_sc = sb("o_sc", [P, S], U8)
+        o_bf = [sb("o_bf%d" % h, [P, W, T4], BF16) for h in range(2)]
+        share = 112
+        nc.vector.tensor_copy(woven_out(o_bf[0][:]), woven(o_all[:, :, :W]))
+        nc.scalar.activation(o_bf[1][:, share:, :], o_all[:, :, W + share:].rearrange("p t c -> p c t"), COPY)
+        nc.vector.tensor_copy(woven_out(o_bf[1][:, :share, :]), woven(o_all[:, :, W:W + share]))
+        o_wd, o_sc = quantize("o", o_bf)
         words_out = out_1[0].rearrange("p c r -> p (c r)").bitcast(I32)
-        for cols in reversed(parts):
-            nc.vector.quantize_mx(out=o_wd[:, cols].bitcast(FP8X4), scales=o_sc[:, cols], in_=o_bf[:, cols, :].rearrange("p c t -> p (c t)"))
-        nc.scalar.dma_start(words_out, o_wd[:].bitcast(I32))
+        for h in range(2):
+            nc.scalar.dma_start(words_out[:, halves[h]], o_wd[:, halves[h]].bitcast(I32))
         for r in range(4):
             nc.sync.dma_start(out_2[0, r:16:4, :].bitcast(I32), o_sc[r:P:32, :].bitcast(I32))

from contextlib import ExitStack

import concourse.mybir as mybir

F32 = mybir.dt.float32
BF16 = mybir.dt.bfloat16
I32 = mybir.dt.int32
U32 = mybir.dt.uint32
U16 = mybir.dt.uint16
U8 = mybir.dt.uint8
FP8X4 = mybir.dt.float8_e4m3fn_x4
FP4X4 = mybir.dt.float4_e2m1fn_x4
ADD = mybir.AluOpType.add
SUB = mybir.AluOpType.subtract
MULT = mybir.AluOpType.mult
COPY = mybir.ActivationFunctionType.Copy

P = 128
T4 = 4
T, S, G, W = 1024, 512, 2048, 256
FLOPS = 3 * 2 * 512 * 512 * 512


def tile_picked_cdkeyputbquadsum_none_po_kernel(
    tc, x_words, x_scales, w1_words, w1_scales, gs, gk, d_words, d_scales,
    offs, n1, n2, n3, n4, cand, k1, n5, n6, out_0, out_1, out_2,
):
    nc = tc.nc
    with ExitStack() as ctx:
        pool = ctx.enter_context(tc.tile_pool(name="held", bufs=1))
        psum = ctx.enter_context(tc.psum_pool(name="psum", bufs=1))

        def sb(name, shape, dtype, tag=None):
            return pool.tile(shape, dtype, name=name, tag=tag or name, align_bytes=64)

        def load_list(name, src):
            lst = pool.tile(list(src.shape), U16, name=name)
            nc.sync.dma_start(lst[:], src)
            return lst

        def load_scales(dst, src):
            for r in range(4):
                nc.sync.dma_start(dst[r:P:32, :].bitcast(I32), src[0, r:16:4, :].bitcast(I32))

        x_sc = sb("x_sc", [P, T], U8)
        w_sc = sb("w_sc", [P, S], U8)
        d_sc = sb("d_sc", [P, G], U8)
        key_sc = sb("key_sc", [P, S], U8)
        nc.gpsimd.memset(x_sc[:].bitcast(I32), 0)
        nc.gpsimd.memset(w_sc[:].bitcast(I32), 0)
        nc.gpsimd.memset(d_sc[:].bitcast(I32), 0)
        nc.gpsimd.memset(key_sc[:].bitcast(I32), 0)

        offs_l = load_list("offs_l", offs)
        w_wd = sb("w_wd", [P, 2 * S], U8)
        nc.sync.dma_start(w_wd[:].bitcast(I32), w1_words[0].bitcast(I32))
        load_scales(x_sc, x_scales)
        x_wd = sb("x_wd", [P, T], U32)
        nc.sync.dma_start(x_wd[:].bitcast(I32), x_words[0].rearrange("p c r -> p (c r)").bitcast(I32))
        load_scales(w_sc, w1_scales)
        cand_l = load_list("cand_l", cand)
        gs4 = sb("gs4", [P, T4], F32)
        gk4 = sb("gk4", [P, T4], F32)
        nc.sync.dma_start(gs4[:], gs.rearrange("(p t) o -> p (t o)", t=T4))
        nc.sync.dma_start(gk4[:], gk.rearrange("(p t) o -> p (t o)", t=T4))
        k1_l = load_list("k1_l", k1)
        for e in range(2):
            nc.sync.dma_start(d_sc[e:P:16, :].bitcast(I32), d_scales[0, e:16:2, :].bitcast(I32))
        n1_l = load_list("n1_l", n1)
        n2_l = load_list("n2_l", n2)
        n3_l = load_list("n3_l", n3)
        n4_l = load_list("n4_l", n4)
        d_wd = sb("d_wd", [P, G], U32)
        nc.sync.dma_start(d_wd[:].bitcast(I32), d_words[0].rearrange("p c r -> p (c r)").bitcast(I32))
        n5_l = load_list("n5_l", n5)
        n6_l = load_list("n6_l", n6)

        gs75 = sb("gs75", [P, T4], F32)
        nc.gpsimd.tensor_scalar(gs75[:], gs4[:], 0.75, 0.0, MULT, ADD)

        def gather(name, window, lst, dtype, tag=None):
            got = sb(name, [P, S], dtype, tag)
            nc.vector.tensor_copy(got[:], window[:].indirect(lst[:]))
            return got

        def deal_words(name, src):
            dst = sb(name, [P, S], U32)
            nc.vector.tensor_copy(dst[:].rearrange("p (t m) -> p m t", t=T4), src[:].rearrange("p (m t) -> p m t", t=T4))
            return dst

        def deal_bytes(name, src):
            dst = sb(name, [P, S], U8)
            nc.vector.tensor_copy(dst[:].rearrange("p (t m) -> p t m", t=T4), src[:].rearrange("p (m t) -> p t m", t=T4))
            return dst

        xq_sc = gather("xq_sc", x_sc, offs_l, U8)
        xq_wd = gather("xq_wd", x_wd, offs_l, U32)
        y_ps = [psum.tile([P, S], F32, name="y_ps%d" % t, tag="low%d" % t) for t in range(T4)]
        for t in range(T4):
            w_wd_t = sb("w_wd_%d" % t, [P, 2 * P], U8)
            w_sc_t = sb("w_sc_%d" % t, [P, P], U8)
            nc.vector.tensor_copy(w_wd_t[:].rearrange("p (m b) -> p m b", b=2), w_wd[:].rearrange("p (m t b) -> p t m b", t=T4, b=2)[:, t])
            nc.vector.tensor_copy(w_sc_t[:], w_sc[:, t:S:T4])
            nc.tensor.matmul_mx(
                out=y_ps[t][:], lhsT=w_wd_t[:].bitcast(FP4X4), lhsT_scale=w_sc_t[:],
                rhs=xq_wd[:].bitcast(FP8X4), rhs_scale=xq_sc[:], start=True, stop=True)

        y_ys = [sb("y_ys%d" % t, [P, 2 * S], F32) for t in range(T4)]
        ys_y = [sb("ys_y%d" % t, [P, 2 * S], F32) for t in range(T4)]
        yk = [sb("yk%d" % t, [P, S + 16], F32) for t in range(T4)]
        ys2 = [sb("ys2_0", [P, S], F32)[:]] + [y_ys[t][:, S:] for t in range(1, T4)]
        nc.gpsimd.memset(y_ys[0][:, S:], 0.0)
        for t in range(T4):
            nc.gpsimd.memset(yk[t][:, S:], 0.0)
        for t in range(T4):
            nc.scalar.activation(y_ys[t][:, :S], y_ps[t][:], COPY)
            nc.sync.dma_start(ys_y[t][:, S:], y_ys[t][:, :S])
            nc.scalar.activation(ys_y[t][:, :S], y_ps[t][:], COPY, scale=gs75[:, t:t + 1])
            nc.sync.dma_start(ys2[t], ys_y[t][:, :S])
        for t in range(T4):
            nc.scalar.activation(yk[t][:, :S], y_ps[t][:], COPY, scale=gk4[:, t:t + 1])

        cand_sc = deal_bytes("cand_sc", gather("cand_sc_g", x_sc, cand_l, U8))
        cand_wd = deal_words("cand_wd", gather("cand_wd_g", x_wd, cand_l, U32))

        key_sc_d = deal_bytes("key_sc_d", gather("key_sc_g", d_sc, k1_l, U8))
        for i, src in enumerate((0, 1, 16, 17)):
            nc.sync.dma_start(key_sc[i:P:32, :].bitcast(I32), key_sc_d[src:P:32, :].bitcast(I32))

        d1 = sb("d1", [P, T4, S], F32)
        d2 = sb("d2", [P, T4, S], F32)
        g3 = sb("g3", [P, T4, S], F32)
        g4 = sb("g4", [P, T4, S], F32)
        for t in range(T4):
            nc.vector.tensor_tensor(d2[:, t, :], y_ys[t][:].indirect(n2_l[:]), ys_y[t][:, S:], SUB)
            nc.vector.tensor_tensor(d1[:, t, :], ys_y[t][:].indirect(n1_l[:]), ys2[t], SUB)
        for t in range(T4):
            nc.scalar.activation(g3[:, t, :], yk[t][:].indirect(n3_l[:]), COPY)
            nc.scalar.activation(g4[:, t, :], yk[t][:].indirect(n4_l[:]), COPY, scale=0.75)

        def woven(planes):
            return planes.rearrange("p t (c i) -> p c t i", i=4)

        def woven_out(words):
            return words.rearrange("p (c i) t -> p c t i", i=4)

        halves = [slice(W * h, W * (h + 1)) for h in range(2)]

        def weave(name, tags, in0, in1, op):
            out = [sb("%s%d" % (name, h), [P, W, T4], BF16, tags[h]) for h in range(2)]
            for h in range(2):
                nc.vector.tensor_tensor(woven_out(out[h][:]), woven(in0[:, :, halves[h]]), woven(in1[:, :, halves[h]]), op)
            return out

        def quantize(name, src):
            wd = sb(name + "_wd", [P, S], U32)
            sc = sb(name + "_sc", [P, S], U8)
            for h in range(2):
                nc.vector.quantize_mx(out=wd[:, halves[h]].bitcast(FP8X4), scales=sc[:, halves[h]], in_=src[h][:].rearrange("p c t -> p (c t)"))
            return wd, sc

        def product(name, tag, lw, ls, rw, rs):
            res = [psum.tile([P, S], F32, name="%s%d" % (name, t), tag="%s%d" % (tag, t)) for t in range(T4)]
            for t in range(T4):
                cols = slice(P * t, P * (t + 1))
                for n in halves:
                    nc.tensor.matmul_mx(out=res[t][:, n], lhsT=lw[:, cols].bitcast(FP8X4), lhsT_scale=ls[:, cols],
                                        rhs=rw[:, n].bitcast(FP8X4), rhs_scale=rs[:, n], start=True, stop=True)
            return res

        z_bf = weave("z_bf", ("z_bf0", "z_bf1"), d1, d2, MULT)
        z_wd, z_sc = quantize("z", z_bf)
        a_ps = product("a_ps", "high", cand_wd, cand_sc, z_wd, z_sc)

        key_wd_g = gather("key_wd_g", d_wd, k1_l, U32, "z_bf0")
        z2_bf = weave("z2_bf", ("z_bf1", "d1"), g3, g4, ADD)
        key_wd = deal_words("key_wd", key_wd_g)
        z2_wd, z2_sc = quantize("z2", z2_bf)
        b_ps = product("b_ps", "low", key_wd, key_sc, z2_wd, z2_sc)

        a_sb = [sb("a_sb%d" % t, [P, S], F32) for t in range(T4)]
        b_sb = [sb("b_sb%d" % t, [P, S], F32, "b_sb%d" % (t % 2)) for t in range(T4)]
        half = [sb("half%d" % t, [P, W], F32) for t in range(T4)]
        ra = [sb("ra%d" % t, [P, W], F32) for t in range(T4)]
        last = T4 - 1
        for t in range(last):
            nc.scalar.activation(a_sb[t][:], a_ps[t][:], COPY, scale=0.0625)
            nc.scalar.activation(half[t][:], a_sb[t][:].indirect(n5_l[:]), COPY, scale=0.5)
        nc.vector.tensor_scalar(a_sb[last][:], a_ps[last][:], 0.0625, None, MULT)
        nc.scalar.activation(b_sb[0][:], b_ps[0][:], COPY, scale=0.0625)
        nc.scalar.activation(half[last][:], a_sb[last][:].indirect(n5_l[:]), COPY, scale=0.5)
        o_all = sb("o_all", [P, T4, S], F32)
        out_rows = out_0.rearrange("(p t) c -> p t c", t=T4)
        for t in range(T4):
            if t > 0:
                nc.vector.tensor_scalar(b_sb[t][:], b_ps[t][:], 0.0625, None, MULT)
            nc.vector.tensor_tensor(ra[t][:], b_sb[t][:].indirect(n6_l[:]), half[t][:], SUB)
        for t in range(T4):
            if t < 3:
                nc.scalar.activation(a_sb[t][:].indirect(n5_l[:]), ra[t][:], COPY)
            else:
                nc.vector.tensor_copy(a_sb[t][:].indirect(n5_l[:]), ra[t][:])
            if t < 2:
                nc.sync.dma_start(o_all[:, t, :], a_sb[t][:])
            nc.sync.dma_start(out_rows[:, t, :], a_sb[t][:])
        for t in (3, 2):
            nc.vector.tensor_copy(o_all[:, t, :], a_sb[t][:])

        o_bf = [sb("o_bf%d" % h, [P, W, T4], BF16) for h in range(2)]
        share = 112
        nc.vector.tensor_copy(woven_out(o_bf[0][:]), woven(o_all[:, :, :W]))
        nc.scalar.activation(o_bf[1][:, share:, :], o_all[:, :, W + share:].rearrange("p t c -> p c t"), COPY)
        nc.vector.tensor_copy(woven_out(o_bf[1][:, :share, :]), woven(o_all[:, :, W:W + share]))
        o_wd, o_sc = quantize("o", o_bf)
        words_out = out_1[0].rearrange("p c r -> p (c r)").bitcast(I32)
        for h in range(2):
            nc.scalar.dma_start(words_out[:, halves[h]], o_wd[:, halves[h]].bitcast(I32))
        for r in range(4):
            nc.sync.dma_start(out_2[0, r:16:4, :].bitcast(I32), o_sc[r:P:32, :].bitcast(I32))
